import numpy as np
import ml_dtypes


def mxq(x, axis, fmt="e4m3"):
    dtype, down = {"e4m3": (ml_dtypes.float8_e4m3fn, 7), "e5m2": (ml_dtypes.float8_e5m2, 14)}[fmt]
    v = np.moveaxis(np.asarray(x, np.float32).astype(ml_dtypes.bfloat16).astype(np.float64), axis, -1)
    blocks = v.reshape(v.shape[:-1] + (-1, 32))
    amax = np.abs(blocks).max(-1, keepdims=True)
    byte = np.maximum(np.where(amax > 0, np.frexp(amax)[1] - 1 + 127, 0) - down, 1)
    scale = np.exp2(byte - 127.0)
    codes = (blocks / scale).astype(np.float32).astype(dtype).astype(np.float64)
    return np.moveaxis((codes * scale).reshape(v.shape), -1, axis)


WIDE = False


def mx_kscale(k):
    if not WIDE:
        return np.ones(k)
    levels = np.array([10, -10, 5, -5, 0])
    if k % 512:
        return np.exp2(np.random.permutation(np.resize(levels, k // 32))).repeat(32)
    a = np.empty((k // 512, 16))
    for p in range(k // 512):
        a[p, :8] = np.random.permutation(np.resize(levels, 8))
        for g in range(8):
            far = levels[np.abs(levels - a[p, g]) >= 10]
            a[p, g + 8] = far[np.random.randint(len(far))]
    return np.exp2(a.ravel()).repeat(32)


def f64(x):
    return np.asarray(x).astype(np.float64)


def striped(idx):
    return np.tile(idx.reshape(-1, 16).T, (8, 1)).astype(np.uint16)


def unstriped(offs):
    return offs[:16].T.reshape(-1).astype(np.int64)


def pack_weight(w):
    k, n = w.shape
    w = f64(np.asarray(w, np.float32).astype(ml_dtypes.bfloat16)).reshape(k // 32, 32, n)
    amax = np.abs(w).max(1)
    byte = np.clip(np.where(amax > 0, np.frexp(amax)[1] - 1 + 127 - 7, 1), 1, 254)
    scaled = (w * np.exp2(127.0 - byte)[:, None, :]).reshape(k, n).astype(np.float32)
    words = np.ascontiguousarray(scaled.reshape(k // 512, 128, 4, n).transpose(0, 1, 3, 2)).astype(ml_dtypes.float8_e4m3fn).view(np.uint8)
    return words, np.ascontiguousarray(byte.astype(np.uint8).reshape(k // 512, 16, n))


def unpack_weight(words, scales):
    g, p, n, _ = words.shape
    vals = np.ascontiguousarray(words).view(ml_dtypes.float8_e4m3fn).astype(np.float64) * np.repeat(np.exp2(scales.astype(np.float64) - 127.0), 8, axis=1)[..., None]
    return vals.transpose(0, 1, 3, 2).reshape(g * 512, n)


E2M1 = np.array([0.0, 0.5, 1.0, 1.5, 2.0, 3.0, 4.0, 6.0, -0.0, -0.5, -1.0, -1.5, -2.0, -3.0, -4.0, -6.0])


def pack_fp4(w):
    k, n = w.shape
    w = f64(np.asarray(w, np.float32).astype(ml_dtypes.bfloat16)).reshape(k // 32, 32, n)
    amax = np.abs(w).max(1)
    mant, ex = np.frexp(amax / 6.0)
    byte = np.clip(np.where(amax > 0, np.where(mant > 0.5, ex, ex - 1) + 127, 1), 1, 254)
    scaled = (w * np.exp2(127.0 - byte)[:, None, :]).reshape(k, n).astype(np.float32)
    c = np.ascontiguousarray(scaled.reshape(k // 512, 128, 4, n).transpose(0, 1, 3, 2)).astype(ml_dtypes.float4_e2m1fn).view(np.uint8) & 0xF
    words = (c[..., 0::2] | (c[..., 1::2] << 4)).reshape(k // 512, 128, 2 * n)
    return np.ascontiguousarray(words), np.ascontiguousarray(byte.astype(np.uint8).reshape(k // 512, 16, n))


def unpack_fp4(words, scales):
    g, _, n = scales.shape
    words = np.ascontiguousarray(words).reshape(g, 128, n, 2)
    nib = np.empty((g, 128, n, 4), np.uint8)
    nib[..., 0::2] = words & 0xF
    nib[..., 1::2] = words >> 4
    vals = E2M1[nib] * np.repeat(np.exp2(scales.astype(np.float64) - 127.0), 8, axis=1)[..., None]
    return vals.transpose(0, 1, 3, 2).reshape(g * 512, n)


def gelu(v):
    return 0.5 * v * (1.0 + np.tanh(np.sqrt(2.0 / np.pi) * (v + 0.044715 * v**3)))


K, T, S, W, H, N = 1024, 2048, 512, 1024, 512, 512


def setup_inputs():
    n = np.random.standard_normal
    s = mx_kscale(K)[:, None]
    u = mx_kscale(H)
    packed_xT = pack_weight(n((K, T)) * s)
    packed_eT = pack_weight(n((K, W)) * s)
    packed_w3 = pack_fp4(n((H, N)) / np.sqrt(H) / u[:, None])
    return {
        "x_words": packed_xT[0],
        "x_scales": packed_xT[1],
        "e_words": packed_eT[0],
        "e_scales": packed_eT[1],
        "w1": (n((K, H)) / np.sqrt(2 * K) / s * u).astype(np.float32),
        "w2": (n((K, H)) / np.sqrt(2 * K) / s * u).astype(np.float32),
        "w3_words": packed_w3[0],
        "w3_scales": packed_w3[1],
        "skip": (n((N, S))).astype(np.float32),
        "offs": striped(np.random.permutation(T)[:S]),
        "tok": striped(np.random.permutation(W)[:S]),
    }


def reference(x_words, x_scales, e_words, e_scales, w1, w2, w3_words, w3_scales, skip, offs, tok):
    xq = unpack_weight(x_words, x_scales)[:, unstriped(offs)]
    e_tok = unpack_weight(e_words, e_scales)[:, unstriped(tok)]
    h = gelu(mxq(f64(w1), 0, "e4m3").T @ xq + mxq(f64(w2), 0, "e4m3").T @ e_tok)
    y = unpack_fp4(w3_words, w3_scales).T @ mxq(h, 0, "e4m3")
    return y + f64(skip)

@@ -1,0 +1,188 @@
+from contextlib import ExitStack
+
+import concourse.mybir as mybir
+from concourse.masks import make_identity
+
+K, T, S, W, H, N = 1024, 2048, 512, 1024, 512, 512
+FLOPS = 2 * (2 * K * H * S + H * N * S)
+
+F32 = mybir.dt.float32
+BF16 = mybir.dt.bfloat16
+I32 = mybir.dt.int32
+U32 = mybir.dt.uint32
+U16 = mybir.dt.uint16
+U8 = mybir.dt.uint8
+FP8X4 = mybir.dt.float8_e4m3fn_x4
+FP4X4 = mybir.dt.float4_e2m1fn_x4
+GELU = mybir.ActivationFunctionType.Gelu_apprx_tanh
+ADD = mybir.AluOpType.add
+
+P = 128
+PACK = 4
+K_PASS = P * PACK
+QUADS = 4
+CHUNKS = S // P
+HALF = H // 2
+
+
+def tile_picked_zeagle_gelu_p_kernel(
+    tc, x_words, x_scales, e_words, e_scales, w1, w2, w3_words, w3_scales, skip, offs, tok, out
+):
+    nc = tc.nc
+    with ExitStack() as ctx:
+        keep = ctx.enter_context(tc.tile_pool(name="keep", bufs=1))
+        psum = ctx.enter_context(tc.psum_pool(name="psum", bufs=1))
+
+        def tile(name, shape, dtype):
+            return keep.tile(shape, dtype, name=name, align_bytes=64)
+
+        offs_sb = keep.tile([P, S // 16], U16, name="offs_sb")
+        tok_sb = keep.tile([P, S // 16], U16, name="tok_sb")
+        x_plane = tile("x_plane", [P, T], U8)
+        e_plane = tile("e_plane", [P, W], U8)
+        w3_plane = tile("w3_plane", [P, N], U8)
+        nc.gpsimd.memset(x_plane[:].bitcast(I32), 0)
+        nc.vector.memset(e_plane[:].bitcast(I32), 0)
+        nc.vector.memset(w3_plane[:].bitcast(I32), 0)
+
+        ident = tile("ident", [P, P], F32)
+        make_identity(nc, ident[:])
+
+        passes = [(w1, x_words, 0, T, offs_sb, 0, 1), (w2, e_words, 0, W, tok_sb, 8, 2),
+                  (w1, x_words, 1, T, offs_sb, 4, 2), (w2, e_words, 1, W, tok_sb, 12, 4)]
+
+        w_raw = [tile("w_raw%d" % g, [P, PACK, H], F32) for g in range(4)]
+        table = [tile("table%d" % g, [P, passes[g][3]], I32) for g in range(4)]
+
+        def load_w(g):
+            w, o = passes[g][0], passes[g][2]
+            nc.sync.dma_start(
+                out=w_raw[g][:], in_=w[o * K_PASS : (o + 1) * K_PASS, :].rearrange("(p t) c -> p t c", t=PACK)
+            )
+
+        def load_table(g):
+            words, o = passes[g][1], passes[g][2]
+            nc.sync.dma_start(out=table[g][:], in_=words[o].rearrange("p n t -> p (n t)").bitcast(I32))
+
+        load_w(0)
+        load_w(1)
+        nc.sync.dma_start(offs_sb[:], offs)
+        nc.sync.dma_start(tok_sb[:], tok)
+        for q in range(QUADS):
+            nc.sync.dma_start(
+                out=x_plane[32 * q : 32 * q + 8, :].bitcast(I32), in_=x_scales[:, 4 * q : 4 * q + 4, :].bitcast(I32)
+            )
+        load_w(2)
+        load_table(0)
+        for q in range(QUADS):
+            nc.sync.dma_start(
+                out=e_plane[32 * q + 8 : 32 * q + 16, :].bitcast(I32),
+                in_=e_scales[:, 4 * q : 4 * q + 4, :].bitcast(I32),
+            )
+        load_w(3)
+        load_table(1)
+        for q in range(QUADS):
+            nc.sync.dma_start(
+                out=w3_plane[32 * q : 32 * q + 4, :].bitcast(I32), in_=w3_scales[0, 4 * q : 4 * q + 4, :].bitcast(I32)
+            )
+        load_table(2)
+        load_table(3)
+        w3_sb = tile("w3_sb", [P, 2 * N], U8)
+        nc.sync.dma_start(out=w3_sb[:].bitcast(I32), in_=w3_words[0].bitcast(I32))
+        skip_sb = tile("skip_sb", [P, N // P, S], F32)
+        nc.sync.dma_start(out=skip_sb[:], in_=skip.rearrange("(m p) j -> p m j", p=P))
+
+        w_codes = [tile("w_codes%d" % g, [P, H], U32) for g in range(4)]
+        w_plane = [tile("w_plane%d" % g, [P, H], U8) for g in range(4)]
+        for g in range(4):
+            halves = []
+            for half, copy in enumerate((nc.scalar.copy, nc.vector.tensor_copy)):
+                cols = slice(half * HALF, (half + 1) * HALF)
+                grouped = tile("w_grouped%d_%d" % (g, half), [P, HALF, PACK], BF16)
+                copy(
+                    out=grouped[:].rearrange("p (c i) t -> p c t i", i=4),
+                    in_=w_raw[g][:, :, cols].rearrange("p t (c i) -> p c t i", i=4),
+                )
+                halves.append((cols, grouped))
+            for cols, grouped in reversed(halves):
+                nc.vector.quantize_mx(
+                    out=w_codes[g][:, cols].bitcast(FP8X4),
+                    scales=w_plane[g][:, cols],
+                    in_=grouped[:].rearrange("p c t -> p (c t)"),
+                )
+
+        x_picked_plane = tile("x_picked_plane", [P, S], U8)
+        e_picked_plane = tile("e_picked_plane", [P, S], U8)
+        nc.vector.tensor_copy(x_picked_plane[:], x_plane[:].indirect(offs_sb[:]))
+        nc.vector.tensor_copy(e_picked_plane[:], e_plane[:].indirect(tok_sb[:]))
+        picked_plane = [x_picked_plane, e_picked_plane, x_picked_plane, e_picked_plane]
+
+        acc = [psum.tile([P, H], F32, name="acc%d" % c, tag="bank%d" % c) for c in range(CHUNKS)]
+        picked = [tile("picked%d" % g, [P, S], U32) for g in range(4)]
+
+        def gather(g):
+            lst, pieces = passes[g][4], passes[g][6]
+            width = S // pieces
+            for piece in range(pieces):
+                nc.vector.tensor_copy(
+                    picked[g][:, piece * width : (piece + 1) * width],
+                    table[g][:].bitcast(U32).indirect(lst[:, piece * width // 16 : (piece + 1) * width // 16]),
+                )
+
+        def multiply(g, c):
+            nodes = slice(c * P, (c + 1) * P)
+            nc.tensor.matmul_mx(
+                out=acc[c][:],
+                lhsT=picked[g][:, nodes].bitcast(FP8X4),
+                lhsT_scale=picked_plane[g][passes[g][5] : P, nodes],
+                rhs=w_codes[g][:].bitcast(FP8X4),
+                rhs_scale=w_plane[g][:],
+                start=(g == 0),
+                stop=(g == 3),
+            )
+
+        for g in range(2):
+            gather(g)
+            for c in range(CHUNKS):
+                multiply(g, c)
+        gather(2)
+        gather(3)
+        for c in range(CHUNKS):
+            multiply(2, c)
+            multiply(3, c)
+
+        hr = []
+        out_view = out.rearrange("(m p) j -> p m j", p=P)
+        for c in range(CHUNKS):
+            nodes = slice(c * P, (c + 1) * P)
+            h_rows = tile("h_rows%d" % c, [P, 2, P, 2], BF16)
+            nc.scalar.activation(h_rows[:], acc[c][:].rearrange("j (p u e) -> j u p e", u=2, e=2), GELU)
+            hr.append(h_rows)
+            h_words = h_rows[:].rearrange("j u p e -> j (u p e)").bitcast(F32)
+            turned = psum.tile([P, 2, P], F32, name="turned%d" % c, tag="turn%d" % c)
+            for u in range(2):
+                nc.tensor.transpose(turned[:, u, :], h_words[:, u * P : (u + 1) * P], ident[:])
+            h_grouped = tile("h_grouped%d" % c, [P, P, 2], F32)
+            copy = nc.vector.tensor_copy if c < 2 else nc.scalar.copy
+            copy(out=h_grouped[:], in_=turned[:].rearrange("p u j -> p j u"))
+            h_codes = tile("h_codes%d" % c, [P, P], U32)
+            h_plane = tile("h_plane%d" % c, [P, P], U8)
+            nc.vector.quantize_mx(
+                out=h_codes[:].bitcast(FP8X4),
+                scales=h_plane[:],
+                in_=h_grouped[:].rearrange("p j u -> p (j u)").bitcast(BF16),
+            )
+            y = psum.tile([P, N // P, P], F32, name="y%d" % c, tag="bank%d" % c)
+            for m in range(N // P):
+                nc.tensor.matmul_mx(
+                    out=y[:, m, :],
+                    lhsT=w3_sb[:, 2 * P * m : 2 * P * (m + 1)].bitcast(FP4X4),
+                    lhsT_scale=w3_plane[:, m * P : (m + 1) * P],
+                    rhs=h_codes[:].bitcast(FP8X4),
+                    rhs_scale=h_plane[:],
+                    start=True,
+                    stop=True,
+                )
+            result = tile("result%d" % c, [P, N // P, P], F32)
+            nc.vector.tensor_tensor(result[:], y[:], skip_sb[:, :, nodes], ADD)
+            nc.sync.dma_start(out=out_view[:, :, nodes], in_=result[:])

@@ -45,6 +45,15 @@ def tile_picked_zeagle_gelu_p_kernel(
         nc.vector.memset(e_plane[:].bitcast(I32), 0)
         nc.vector.memset(w3_plane[:].bitcast(I32), 0)
 
+        for q in range(QUADS):
+            nc.gpsimd.dma_start(
+                out=x_plane[32 * q : 32 * q + 8, :].bitcast(I32), in_=x_scales[:, 4 * q : 4 * q + 4, :].bitcast(I32)
+            )
+        for q in range(QUADS):
+            nc.gpsimd.dma_start(
+                out=e_plane[32 * q + 8 : 32 * q + 16, :].bitcast(I32),
+                in_=e_scales[:, 4 * q : 4 * q + 4, :].bitcast(I32),
+            )
         ident = tile("ident", [P, P], F32)
         make_identity(nc, ident[:])
 
@@ -68,25 +77,16 @@ def tile_picked_zeagle_gelu_p_kernel(
         load_w(1)
         nc.sync.dma_start(offs_sb[:], offs)
         nc.sync.dma_start(tok_sb[:], tok)
-        for q in range(QUADS):
-            nc.sync.dma_start(
-                out=x_plane[32 * q : 32 * q + 8, :].bitcast(I32), in_=x_scales[:, 4 * q : 4 * q + 4, :].bitcast(I32)
-            )
         load_w(2)
         load_table(0)
-        for q in range(QUADS):
-            nc.sync.dma_start(
-                out=e_plane[32 * q + 8 : 32 * q + 16, :].bitcast(I32),
-                in_=e_scales[:, 4 * q : 4 * q + 4, :].bitcast(I32),
-            )
         load_w(3)
         load_table(1)
+        load_table(2)
+        load_table(3)
         for q in range(QUADS):
             nc.sync.dma_start(
                 out=w3_plane[32 * q : 32 * q + 4, :].bitcast(I32), in_=w3_scales[0, 4 * q : 4 * q + 4, :].bitcast(I32)
             )
-        load_table(2)
-        load_table(3)
         w3_sb = tile("w3_sb", [P, 2 * N], U8)
         nc.sync.dma_start(out=w3_sb[:].bitcast(I32), in_=w3_words[0].bitcast(I32))
         skip_sb = tile("skip_sb", [P, N // P, S], F32)
@@ -184,5 +184,9 @@ def tile_picked_zeagle_gelu_p_kernel(
                     stop=True,
                 )
             result = tile("result%d" % c, [P, N // P, P], F32)
-            nc.vector.tensor_tensor(result[:], y[:], skip_sb[:, :, nodes], ADD)
-            nc.sync.dma_start(out=out_view[:, :, nodes], in_=result[:])
+            parts = 2 if c == CHUNKS - 1 else 1
+            rows = N // P // parts
+            for part in range(parts):
+                ms = slice(part * rows, (part + 1) * rows)
+                nc.vector.tensor_tensor(result[:, ms, :], y[:, ms, :], skip_sb[:, ms, nodes], ADD)
+                nc.sync.dma_start(out=out_view[:, ms, nodes], in_=result[:, ms, :])

@@ -45,20 +45,11 @@ def tile_picked_zeagle_gelu_p_kernel(
         nc.vector.memset(e_plane[:].bitcast(I32), 0)
         nc.vector.memset(w3_plane[:].bitcast(I32), 0)
 
-        for q in range(QUADS):
-            nc.gpsimd.dma_start(
-                out=x_plane[32 * q : 32 * q + 8, :].bitcast(I32), in_=x_scales[:, 4 * q : 4 * q + 4, :].bitcast(I32)
-            )
-        for q in range(QUADS):
-            nc.gpsimd.dma_start(
-                out=e_plane[32 * q + 8 : 32 * q + 16, :].bitcast(I32),
-                in_=e_scales[:, 4 * q : 4 * q + 4, :].bitcast(I32),
-            )
         ident = tile("ident", [P, P], F32)
         make_identity(nc, ident[:])
 
-        passes = [(w1, x_words, 0, T, offs_sb, 0, 1), (w2, e_words, 0, W, tok_sb, 8, 2),
-                  (w1, x_words, 1, T, offs_sb, 4, 2), (w2, e_words, 1, W, tok_sb, 12, 4)]
+        passes = [(w1, x_words, 0, T, offs_sb, 0, 1), (w2, e_words, 0, W, tok_sb, 8, 4),
+                  (w2, e_words, 1, W, tok_sb, 12, 2), (w1, x_words, 1, T, offs_sb, 4, 2)]
 
         w_raw = [tile("w_raw%d" % g, [P, PACK, H], F32) for g in range(4)]
         table = [tile("table%d" % g, [P, passes[g][3]], I32) for g in range(4)]
@@ -73,24 +64,36 @@ def tile_picked_zeagle_gelu_p_kernel(
             words, o = passes[g][1], passes[g][2]
             nc.sync.dma_start(out=table[g][:], in_=words[o].rearrange("p n t -> p (n t)").bitcast(I32))
 
+        def load_scale_rows(plane, first, scales, r):
+            nc.sync.dma_start(
+                out=plane[first + r : P : 32, :].bitcast(I32), in_=scales[r : 16 : QUADS, :].bitcast(I32)
+            )
+
+        rows = [(x_plane, 4 * o, x_scales[o], r) for o in range(2) for r in range(4)]
+        rows = rows + [(e_plane, 8 + 4 * o, e_scales[o], r) for o in range(2) for r in range(4)]
         load_w(0)
-        load_w(1)
         nc.sync.dma_start(offs_sb[:], offs)
         nc.sync.dma_start(tok_sb[:], tok)
-        load_w(2)
-        load_table(0)
+        for g, load in enumerate((load_w, load_w, load_table)):
+            for row in rows[4 * g : 4 * g + 4]:
+                load_scale_rows(*row)
+            load((g + 1) % 3)
+        for row in rows[12:16]:
+            load_scale_rows(*row)
         load_w(3)
+        for r in range(2):
+            load_scale_rows(w3_plane, 0, w3_scales[0], r)
         load_table(1)
+        for r in range(2, 4):
+            load_scale_rows(w3_plane, 0, w3_scales[0], r)
         load_table(2)
         load_table(3)
-        for q in range(QUADS):
-            nc.sync.dma_start(
-                out=w3_plane[32 * q : 32 * q + 4, :].bitcast(I32), in_=w3_scales[0, 4 * q : 4 * q + 4, :].bitcast(I32)
-            )
         w3_sb = tile("w3_sb", [P, 2 * N], U8)
         nc.sync.dma_start(out=w3_sb[:].bitcast(I32), in_=w3_words[0].bitcast(I32))
-        skip_sb = tile("skip_sb", [P, N // P, S], F32)
-        nc.sync.dma_start(out=skip_sb[:], in_=skip.rearrange("(m p) j -> p m j", p=P))
+        skip_view = skip.rearrange("(m p) j -> p m j", p=P)
+        skip_sb = [tile("skip_sb%d" % half, [P, N // P, S // 2], F32) for half in range(2)]
+        for half in range(2):
+            nc.sync.dma_start(out=skip_sb[half][:], in_=skip_view[:, :, half * S // 2 : (half + 1) * S // 2])
 
         w_codes = [tile("w_codes%d" % g, [P, H], U32) for g in range(4)]
         w_plane = [tile("w_plane%d" % g, [P, H], U8) for g in range(4)]
@@ -115,7 +118,7 @@ def tile_picked_zeagle_gelu_p_kernel(
         e_picked_plane = tile("e_picked_plane", [P, S], U8)
         nc.vector.tensor_copy(x_picked_plane[:], x_plane[:].indirect(offs_sb[:]))
         nc.vector.tensor_copy(e_picked_plane[:], e_plane[:].indirect(tok_sb[:]))
-        picked_plane = [x_picked_plane, e_picked_plane, x_picked_plane, e_picked_plane]
+        picked_plane = [x_picked_plane, e_picked_plane, e_picked_plane, x_picked_plane]
 
         acc = [psum.tile([P, H], F32, name="acc%d" % c, tag="bank%d" % c) for c in range(CHUNKS)]
         picked = [tile("picked%d" % g, [P, S], U32) for g in range(4)]
@@ -141,52 +144,90 @@ def tile_picked_zeagle_gelu_p_kernel(
                 stop=(g == 3),
             )
 
-        for g in range(2):
+        for g in range(4):
             gather(g)
             for c in range(CHUNKS):
                 multiply(g, c)
-        gather(2)
-        gather(3)
-        for c in range(CHUNKS):
-            multiply(2, c)
-            multiply(3, c)
 
-        hr = []
         out_view = out.rearrange("(m p) j -> p m j", p=P)
-        for c in range(CHUNKS):
-            nodes = slice(c * P, (c + 1) * P)
-            h_rows = tile("h_rows%d" % c, [P, 2, P, 2], BF16)
-            nc.scalar.activation(h_rows[:], acc[c][:].rearrange("j (p u e) -> j u p e", u=2, e=2), GELU)
-            hr.append(h_rows)
-            h_words = h_rows[:].rearrange("j u p e -> j (u p e)").bitcast(F32)
-            turned = psum.tile([P, 2, P], F32, name="turned%d" % c, tag="turn%d" % c)
+        h_rows = [tile("h_rows%d" % c, [P, 2, P, 2], BF16) for c in range(CHUNKS)]
+        turned = [psum.tile([P, 2, P], F32, name="turned%d" % c, tag="turn%d" % c) for c in range(CHUNKS)]
+        h_grouped = [tile("h_grouped%d" % c, [P, P, 2], F32) for c in range(CHUNKS)]
+        h_codes = [tile("h_codes%d" % c, [P, P], U32) for c in range(CHUNKS)]
+        h_plane = [tile("h_plane%d" % c, [P, P], U8) for c in range(CHUNKS)]
+        y = {}
+        results = {}
+
+        def gelu(c, parts):
+            view = acc[c][:].rearrange("j (p u e) -> j u p e", u=2, e=2)
+            for part in range(parts):
+                us = slice(part * 2 // parts, (part + 1) * 2 // parts)
+                nc.scalar.activation(h_rows[c][:, us], view[:, us], GELU)
+
+        def turn(c):
+            h_words = h_rows[c][:].rearrange("j u p e -> j (u p e)").bitcast(F32)
             for u in range(2):
-                nc.tensor.transpose(turned[:, u, :], h_words[:, u * P : (u + 1) * P], ident[:])
-            h_grouped = tile("h_grouped%d" % c, [P, P, 2], F32)
-            copy = nc.vector.tensor_copy if c < 2 else nc.scalar.copy
-            copy(out=h_grouped[:], in_=turned[:].rearrange("p u j -> p j u"))
-            h_codes = tile("h_codes%d" % c, [P, P], U32)
-            h_plane = tile("h_plane%d" % c, [P, P], U8)
+                nc.tensor.transpose(turned[c][:, u, :], h_words[:, u * P : (u + 1) * P], ident[:])
+
+        def weave(c, copy):
+            copy(out=h_grouped[c][:], in_=turned[c][:].rearrange("p u j -> p j u"))
+
+        def quantize(c):
             nc.vector.quantize_mx(
-                out=h_codes[:].bitcast(FP8X4),
-                scales=h_plane[:],
-                in_=h_grouped[:].rearrange("p j u -> p (j u)").bitcast(BF16),
+                out=h_codes[c][:].bitcast(FP8X4),
+                scales=h_plane[c][:],
+                in_=h_grouped[c][:].rearrange("p j u -> p (j u)").bitcast(BF16),
             )
-            y = psum.tile([P, N // P, P], F32, name="y%d" % c, tag="bank%d" % c)
-            for m in range(N // P):
-                nc.tensor.matmul_mx(
-                    out=y[:, m, :],
-                    lhsT=w3_sb[:, 2 * P * m : 2 * P * (m + 1)].bitcast(FP4X4),
-                    lhsT_scale=w3_plane[:, m * P : (m + 1) * P],
-                    rhs=h_codes[:].bitcast(FP8X4),
-                    rhs_scale=h_plane[:],
-                    start=True,
-                    stop=True,
-                )
-            result = tile("result%d" % c, [P, N // P, P], F32)
-            parts = 2 if c == CHUNKS - 1 else 1
+
+        def second(c, parts):
+            rows = N // P // parts
+            for part in range(parts):
+                bank = psum.tile([P, rows, P], F32, name="y%d_%d" % (c, part), tag=("bank%d", "turn%d")[part] % c)
+                y.setdefault((c, part), bank)
+                for i in range(rows):
+                    m = part * rows + i
+                    nc.tensor.matmul_mx(
+                        out=bank[:, i, :],
+                        lhsT=w3_sb[:, 2 * P * m : 2 * P * (m + 1)].bitcast(FP4X4),
+                        lhsT_scale=w3_plane[:, m * P : (m + 1) * P],
+                        rhs=h_codes[c][:].bitcast(FP8X4),
+                        rhs_scale=h_plane[c][:],
+                        start=True,
+                        stop=True,
+                    )
+
+        def finish(c, parts):
+            nodes = slice(c * P, (c + 1) * P)
             rows = N // P // parts
             for part in range(parts):
                 ms = slice(part * rows, (part + 1) * rows)
-                nc.vector.tensor_tensor(result[:, ms, :], y[:, ms, :], skip_sb[:, ms, nodes], ADD)
-                nc.sync.dma_start(out=out_view[:, ms, nodes], in_=result[:, ms, :])
+                result = tile("result%d_%d" % (c, part), [P, rows, P], F32)
+                results.setdefault(c, result)
+                nc.vector.tensor_tensor(
+                    result[:], y[(c, part)][:], skip_sb[c // 2][:, ms, c % 2 * P : (c % 2 + 1) * P], ADD
+                )
+                nc.sync.dma_start(out=out_view[:, ms, nodes], in_=result[:])
+
+        V, A = nc.vector.tensor_copy, nc.scalar.copy
+        for c in range(CHUNKS):
+            gelu(c, 2 if c in (0, 3) else 1)
+        turn(0)
+        weave(0, V)
+        turn(1)
+        quantize(0)
+        weave(1, V)
+        turn(2)
+        second(0, 2)
+        quantize(1)
+        weave(2, A)
+        turn(3)
+        weave(3, A)
+        second(1, 1)
+        finish(0, 2)
+        quantize(2)
+        second(2, 1)
+        finish(1, 1)
+        quantize(3)
+        second(3, 2)
+        finish(2, 1)
+        finish(3, 2)

@@ -1,7 +1,6 @@
 from contextlib import ExitStack
 
 import concourse.mybir as mybir
-from concourse.masks import make_identity
 
 K, T, S, W, H, N = 1024, 2048, 512, 1024, 512, 512
 FLOPS = 2 * (2 * K * H * S + H * N * S)
@@ -22,7 +21,7 @@ PACK = 4
 K_PASS = P * PACK
 QUADS = 4
 CHUNKS = S // P
-HALF = H // 2
+SCALAR_SHARE = 80
 
 
 def tile_picked_zeagle_gelu_p_kernel(
@@ -41,15 +40,12 @@ def tile_picked_zeagle_gelu_p_kernel(
         x_plane = tile("x_plane", [P, T], U8)
         e_plane = tile("e_plane", [P, W], U8)
         w3_plane = tile("w3_plane", [P, N], U8)
-        nc.gpsimd.memset(x_plane[:].bitcast(I32), 0)
         nc.vector.memset(e_plane[:].bitcast(I32), 0)
+        nc.vector.memset(x_plane[:].bitcast(I32), 0)
         nc.vector.memset(w3_plane[:].bitcast(I32), 0)
 
-        ident = tile("ident", [P, P], F32)
-        make_identity(nc, ident[:])
-
-        passes = [(w1, x_words, 0, T, offs_sb, 0, 1), (w2, e_words, 0, W, tok_sb, 8, 4),
-                  (w2, e_words, 1, W, tok_sb, 12, 2), (w1, x_words, 1, T, offs_sb, 4, 2)]
+        passes = [(w2, e_words, 0, W, tok_sb, 8, 2), (w1, x_words, 0, T, offs_sb, 0, 2),
+                  (w1, x_words, 1, T, offs_sb, 4, 2), (w2, e_words, 1, W, tok_sb, 12, 4)]
 
         w_raw = [tile("w_raw%d" % g, [P, PACK, H], F32) for g in range(4)]
         table = [tile("table%d" % g, [P, passes[g][3]], I32) for g in range(4)]
@@ -69,18 +65,16 @@ def tile_picked_zeagle_gelu_p_kernel(
                 out=plane[first + r : P : 32, :].bitcast(I32), in_=scales[r : 16 : QUADS, :].bitcast(I32)
             )
 
-        rows = [(x_plane, 4 * o, x_scales[o], r) for o in range(2) for r in range(4)]
-        rows = rows + [(e_plane, 8 + 4 * o, e_scales[o], r) for o in range(2) for r in range(4)]
+        rows = [(e_plane, 8 + 4 * o, e_scales[o], r) for o in range(2) for r in range(4)]
+        rows = rows + [(x_plane, 4 * o, x_scales[o], r) for o in range(2) for r in range(4)]
         load_w(0)
         nc.sync.dma_start(offs_sb[:], offs)
         nc.sync.dma_start(tok_sb[:], tok)
-        for g, load in enumerate((load_w, load_w, load_table)):
-            for row in rows[4 * g : 4 * g + 4]:
+        for g, (first, last) in enumerate(((0, 4), (4, 10), (10, 16))):
+            for row in rows[first:last]:
                 load_scale_rows(*row)
-            load((g + 1) % 3)
-        for row in rows[12:16]:
-            load_scale_rows(*row)
-        load_w(3)
+            load_w(g + 1)
+        load_table(0)
         for r in range(2):
             load_scale_rows(w3_plane, 0, w3_scales[0], r)
         load_table(1)
@@ -98,29 +92,25 @@ def tile_picked_zeagle_gelu_p_kernel(
         w_codes = [tile("w_codes%d" % g, [P, H], U32) for g in range(4)]
         w_plane = [tile("w_plane%d" % g, [P, H], U8) for g in range(4)]
         for g in range(4):
-            halves = []
-            for half, copy in enumerate((nc.scalar.copy, nc.vector.tensor_copy)):
-                cols = slice(half * HALF, (half + 1) * HALF)
-                grouped = tile("w_grouped%d_%d" % (g, half), [P, HALF, PACK], BF16)
+            grouped = tile("w_grouped%d" % g, [P, PACK, P, PACK], BF16)
+            for ms, copy in ((slice(0, SCALAR_SHARE), nc.scalar.copy), (slice(SCALAR_SHARE, P), nc.vector.tensor_copy)):
                 copy(
-                    out=grouped[:].rearrange("p (c i) t -> p c t i", i=4),
-                    in_=w_raw[g][:, :, cols].rearrange("p t (c i) -> p c t i", i=4),
+                    out=grouped[:, :, ms, :].rearrange("p t m j -> p m j t"),
+                    in_=w_raw[g][:].rearrange("p j (m t) -> p m j t", t=PACK)[:, ms],
                 )
-                halves.append((cols, grouped))
-            for cols, grouped in reversed(halves):
-                nc.vector.quantize_mx(
-                    out=w_codes[g][:, cols].bitcast(FP8X4),
-                    scales=w_plane[g][:, cols],
-                    in_=grouped[:].rearrange("p c t -> p (c t)"),
-                )
+            nc.vector.quantize_mx(
+                out=w_codes[g][:].bitcast(FP8X4),
+                scales=w_plane[g][:],
+                in_=grouped[:].rearrange("p t m j -> p (t m j)"),
+            )
 
         x_picked_plane = tile("x_picked_plane", [P, S], U8)
         e_picked_plane = tile("e_picked_plane", [P, S], U8)
-        nc.vector.tensor_copy(x_picked_plane[:], x_plane[:].indirect(offs_sb[:]))
         nc.vector.tensor_copy(e_picked_plane[:], e_plane[:].indirect(tok_sb[:]))
-        picked_plane = [x_picked_plane, e_picked_plane, e_picked_plane, x_picked_plane]
+        nc.vector.tensor_copy(x_picked_plane[:], x_plane[:].indirect(offs_sb[:]))
+        picked_plane = [e_picked_plane, x_picked_plane, x_picked_plane, e_picked_plane]
 
-        acc = [psum.tile([P, H], F32, name="acc%d" % c, tag="bank%d" % c) for c in range(CHUNKS)]
+        acc = [psum.tile([P, PACK, P], F32, name="acc%d" % c, tag="bank%d" % c) for c in range(CHUNKS)]
         picked = [tile("picked%d" % g, [P, S], U32) for g in range(4)]
 
         def gather(g):
@@ -134,55 +124,50 @@ def tile_picked_zeagle_gelu_p_kernel(
 
         def multiply(g, c):
             nodes = slice(c * P, (c + 1) * P)
-            nc.tensor.matmul_mx(
-                out=acc[c][:],
-                lhsT=picked[g][:, nodes].bitcast(FP8X4),
-                lhsT_scale=picked_plane[g][passes[g][5] : P, nodes],
-                rhs=w_codes[g][:].bitcast(FP8X4),
-                rhs_scale=w_plane[g][:],
-                start=(g == 0),
-                stop=(g == 3),
-            )
+            for t in range(PACK):
+                cols = slice(t * P, (t + 1) * P)
+                nc.tensor.matmul_mx(
+                    out=acc[c][:, t, :],
+                    lhsT=w_codes[g][:, cols].bitcast(FP8X4),
+                    lhsT_scale=w_plane[g][:, cols],
+                    rhs=picked[g][:, nodes].bitcast(FP8X4),
+                    rhs_scale=picked_plane[g][passes[g][5] : P, nodes],
+                    start=(g == 0 and t == 0),
+                    stop=(g == 3 and t == PACK - 1),
+                )
 
         for g in range(4):
             gather(g)
+        for g in range(2):
             for c in range(CHUNKS):
                 multiply(g, c)
+        for c in range(CHUNKS + 2):
+            if c < CHUNKS:
+                multiply(2, c)
+            if c >= 2:
+                multiply(3, c - 2)
 
         out_view = out.rearrange("(m p) j -> p m j", p=P)
-        h_rows = [tile("h_rows%d" % c, [P, 2, P, 2], BF16) for c in range(CHUNKS)]
-        turned = [psum.tile([P, 2, P], F32, name="turned%d" % c, tag="turn%d" % c) for c in range(CHUNKS)]
-        h_grouped = [tile("h_grouped%d" % c, [P, P, 2], F32) for c in range(CHUNKS)]
+        h_grouped = [tile("h_grouped%d" % c, [P, P, PACK], BF16) for c in range(CHUNKS)]
         h_codes = [tile("h_codes%d" % c, [P, P], U32) for c in range(CHUNKS)]
         h_plane = [tile("h_plane%d" % c, [P, P], U8) for c in range(CHUNKS)]
         y = {}
         results = {}
 
-        def gelu(c, parts):
-            view = acc[c][:].rearrange("j (p u e) -> j u p e", u=2, e=2)
-            for part in range(parts):
-                us = slice(part * 2 // parts, (part + 1) * 2 // parts)
-                nc.scalar.activation(h_rows[c][:, us], view[:, us], GELU)
-
-        def turn(c):
-            h_words = h_rows[c][:].rearrange("j u p e -> j (u p e)").bitcast(F32)
-            for u in range(2):
-                nc.tensor.transpose(turned[c][:, u, :], h_words[:, u * P : (u + 1) * P], ident[:])
-
-        def weave(c, copy):
-            copy(out=h_grouped[c][:], in_=turned[c][:].rearrange("p u j -> p j u"))
+        def gelu(c):
+            nc.scalar.activation(h_grouped[c][:], acc[c][:].rearrange("p t j -> p j t"), GELU)
 
         def quantize(c):
             nc.vector.quantize_mx(
                 out=h_codes[c][:].bitcast(FP8X4),
                 scales=h_plane[c][:],
-                in_=h_grouped[c][:].rearrange("p j u -> p (j u)").bitcast(BF16),
+                in_=h_grouped[c][:].rearrange("p j t -> p (j t)"),
             )
 
         def second(c, parts):
             rows = N // P // parts
             for part in range(parts):
-                bank = psum.tile([P, rows, P], F32, name="y%d_%d" % (c, part), tag=("bank%d", "turn%d")[part] % c)
+                bank = psum.tile([P, rows, P], F32, name="y%d_%d" % (c, part), tag=("out%d", "bank%d")[part] % c)
                 y.setdefault((c, part), bank)
                 for i in range(rows):
                     m = part * rows + i
@@ -208,20 +193,11 @@ def tile_picked_zeagle_gelu_p_kernel(
                 )
                 nc.sync.dma_start(out=out_view[:, ms, nodes], in_=result[:])
 
-        V, A = nc.vector.tensor_copy, nc.scalar.copy
         for c in range(CHUNKS):
-            gelu(c, 2 if c in (0, 3) else 1)
-        turn(0)
-        weave(0, V)
-        turn(1)
+            gelu(c)
         quantize(0)
-        weave(1, V)
-        turn(2)
         second(0, 2)
         quantize(1)
-        weave(2, A)
-        turn(3)
-        weave(3, A)
         second(1, 1)
         finish(0, 2)
         quantize(2)

@@ -65,8 +65,8 @@ def tile_picked_zeagle_gelu_p_kernel(
                 out=plane[first + r : P : 32, :].bitcast(I32), in_=scales[r : 16 : QUADS, :].bitcast(I32)
             )
 
-        rows = [(e_plane, 8 + 4 * o, e_scales[o], r) for o in range(2) for r in range(4)]
-        rows = rows + [(x_plane, 4 * o, x_scales[o], r) for o in range(2) for r in range(4)]
+        rows = [(e_plane, 8 + 4 * o, e_scales[o], r) for r in range(4) for o in range(2)]
+        rows = rows + [(x_plane, 4 * o, x_scales[o], r) for r in range(4) for o in range(2)]
         load_w(0)
         nc.sync.dma_start(offs_sb[:], offs)
         nc.sync.dma_start(tok_sb[:], tok)

@@ -33,7 +33,7 @@ def tile_picked_zeagle_gelu_p_kernel(
         psum = ctx.enter_context(tc.psum_pool(name="psum", bufs=1))
 
         def tile(name, shape, dtype):
-            return keep.tile(shape, dtype, name=name, align_bytes=64)
+            return keep.tile(shape, dtype, name=name, align_bytes=256)
 
         offs_sb = keep.tile([P, S // 16], U16, name="offs_sb")
         tok_sb = keep.tile([P, S // 16], U16, name="tok_sb")

@@ -33,7 +33,7 @@ def tile_picked_zeagle_gelu_p_kernel(
         psum = ctx.enter_context(tc.psum_pool(name="psum", bufs=1))
 
         def tile(name, shape, dtype):
-            return keep.tile(shape, dtype, name=name, align_bytes=256)
+            return keep.tile(shape, dtype, name=name, align_bytes=1024)
 
         offs_sb = keep.tile([P, S // 16], U16, name="offs_sb")
         tok_sb = keep.tile([P, S // 16], U16, name="tok_sb")

@@ -155,7 +155,11 @@ def tile_picked_zeagle_gelu_p_kernel(
         results = {}
 
         def gelu(c):
-            nc.scalar.activation(h_grouped[c][:], acc[c][:].rearrange("p t j -> p j t"), GELU)
+            nc.scalar.activation(
+                h_grouped[c][:].rearrange("p (j u) t -> p j t u", u=2),
+                acc[c][:].rearrange("p t (j u) -> p j t u", u=2),
+                GELU,
+            )
 
         def quantize(c):
             nc.vector.quantize_mx(

@@ -32,8 +32,8 @@ def tile_picked_zeagle_gelu_p_kernel(
         keep = ctx.enter_context(tc.tile_pool(name="keep", bufs=1))
         psum = ctx.enter_context(tc.psum_pool(name="psum", bufs=1))
 
-        def tile(name, shape, dtype):
-            return keep.tile(shape, dtype, name=name, align_bytes=1024)
+        def tile(name, shape, dtype, tag=None):
+            return keep.tile(shape, dtype, name=name, tag=tag or name, align_bytes=1024)
 
         offs_sb = keep.tile([P, S // 16], U16, name="offs_sb")
         tok_sb = keep.tile([P, S // 16], U16, name="tok_sb")
@@ -44,8 +44,8 @@ def tile_picked_zeagle_gelu_p_kernel(
         nc.vector.memset(x_plane[:].bitcast(I32), 0)
         nc.vector.memset(w3_plane[:].bitcast(I32), 0)
 
-        passes = [(w2, e_words, 0, W, tok_sb, 8, 2), (w1, x_words, 0, T, offs_sb, 0, 2),
-                  (w1, x_words, 1, T, offs_sb, 4, 2), (w2, e_words, 1, W, tok_sb, 12, 4)]
+        passes = [(w2, e_words, 0, W, tok_sb, 8, 2), (w2, e_words, 1, W, tok_sb, 12, 2),
+                  (w1, x_words, 0, T, offs_sb, 0, 2), (w1, x_words, 1, T, offs_sb, 4, 4)]
 
         w_raw = [tile("w_raw%d" % g, [P, PACK, H], F32) for g in range(4)]
         table = [tile("table%d" % g, [P, passes[g][3]], I32) for g in range(4)]
@@ -74,12 +74,10 @@ def tile_picked_zeagle_gelu_p_kernel(
             for row in rows[first:last]:
                 load_scale_rows(*row)
             load_w(g + 1)
-        load_table(0)
-        for r in range(2):
-            load_scale_rows(w3_plane, 0, w3_scales[0], r)
-        load_table(1)
-        for r in range(2, 4):
-            load_scale_rows(w3_plane, 0, w3_scales[0], r)
+        for g in range(2):
+            load_table(g)
+            for r in range(2 * g, 2 * g + 2):
+                load_scale_rows(w3_plane, 0, w3_scales[0], r)
         load_table(2)
         load_table(3)
         w3_sb = tile("w3_sb", [P, 2 * N], U8)
@@ -89,15 +87,17 @@ def tile_picked_zeagle_gelu_p_kernel(
         for half in range(2):
             nc.sync.dma_start(out=skip_sb[half][:], in_=skip_view[:, :, half * S // 2 : (half + 1) * S // 2])
 
-        w_codes = [tile("w_codes%d" % g, [P, H], U32) for g in range(4)]
-        w_plane = [tile("w_plane%d" % g, [P, H], U8) for g in range(4)]
-        for g in range(4):
+        w_codes, w_plane = [], []
+
+        def quantize_w(g, after):
             grouped = tile("w_grouped%d" % g, [P, PACK, P, PACK], BF16)
             for ms, copy in ((slice(0, SCALAR_SHARE), nc.scalar.copy), (slice(SCALAR_SHARE, P), nc.vector.tensor_copy)):
                 copy(
                     out=grouped[:, :, ms, :].rearrange("p t m j -> p m j t"),
                     in_=w_raw[g][:].rearrange("p j (m t) -> p m j t", t=PACK)[:, ms],
                 )
+            w_codes.append(tile("w_codes%d" % g, [P, H], U32, after))
+            w_plane.append(tile("w_plane%d" % g, [P, H], U8))
             nc.vector.quantize_mx(
                 out=w_codes[g][:].bitcast(FP8X4),
                 scales=w_plane[g][:],
@@ -106,10 +106,7 @@ def tile_picked_zeagle_gelu_p_kernel(
 
         x_picked_plane = tile("x_picked_plane", [P, S], U8)
         e_picked_plane = tile("e_picked_plane", [P, S], U8)
-        nc.vector.tensor_copy(e_picked_plane[:], e_plane[:].indirect(tok_sb[:]))
-        nc.vector.tensor_copy(x_picked_plane[:], x_plane[:].indirect(offs_sb[:]))
-        picked_plane = [e_picked_plane, x_picked_plane, x_picked_plane, e_picked_plane]
-
+        picked_plane = [e_picked_plane, e_picked_plane, x_picked_plane, x_picked_plane]
         acc = [psum.tile([P, PACK, P], F32, name="acc%d" % c, tag="bank%d" % c) for c in range(CHUNKS)]
         picked = [tile("picked%d" % g, [P, S], U32) for g in range(4)]
 
@@ -122,30 +119,35 @@ def tile_picked_zeagle_gelu_p_kernel(
                     table[g][:].bitcast(U32).indirect(lst[:, piece * width // 16 : (piece + 1) * width // 16]),
                 )
 
-        def multiply(g, c):
-            nodes = slice(c * P, (c + 1) * P)
-            for t in range(PACK):
-                cols = slice(t * P, (t + 1) * P)
-                nc.tensor.matmul_mx(
-                    out=acc[c][:, t, :],
-                    lhsT=w_codes[g][:, cols].bitcast(FP8X4),
-                    lhsT_scale=w_plane[g][:, cols],
-                    rhs=picked[g][:, nodes].bitcast(FP8X4),
-                    rhs_scale=picked_plane[g][passes[g][5] : P, nodes],
-                    start=(g == 0 and t == 0),
-                    stop=(g == 3 and t == PACK - 1),
-                )
-
-        for g in range(4):
-            gather(g)
-        for g in range(2):
+        def multiply(g):
             for c in range(CHUNKS):
-                multiply(g, c)
-        for c in range(CHUNKS + 2):
-            if c < CHUNKS:
-                multiply(2, c)
-            if c >= 2:
-                multiply(3, c - 2)
+                nodes = slice(c * P, (c + 1) * P)
+                for t in range(PACK):
+                    cols = slice(t * P, (t + 1) * P)
+                    nc.tensor.matmul_mx(
+                        out=acc[c][:, t, :],
+                        lhsT=w_codes[g][:, cols].bitcast(FP8X4),
+                        lhsT_scale=w_plane[g][:, cols],
+                        rhs=picked[g][:, nodes].bitcast(FP8X4),
+                        rhs_scale=picked_plane[g][passes[g][5] : P, nodes],
+                        start=(g == 0 and t == 0),
+                        stop=(g == 3 and t == PACK - 1),
+                    )
+
+        quantize_w(0, None)
+        nc.vector.tensor_copy(e_picked_plane[:], e_plane[:].indirect(tok_sb[:]))
+        quantize_w(1, "e_plane")
+        nc.vector.tensor_copy(x_picked_plane[:], x_plane[:].indirect(offs_sb[:]))
+        quantize_w(2, "x_plane")
+        gather(0)
+        multiply(0)
+        gather(1)
+        multiply(1)
+        quantize_w(3, "table1")
+        gather(2)
+        multiply(2)
+        gather(3)
+        multiply(3)
 
         out_view = out.rearrange("(m p) j -> p m j", p=P)
         h_grouped = [tile("h_grouped%d" % c, [P, P, PACK], BF16) for c in range(CHUNKS)]

@@ -42,9 +42,11 @@ def tile_picked_zeagle_gelu_p_kernel(
         w3_plane = tile("w3_plane", [P, N], U8)
         nc.vector.memset(e_plane[:].bitcast(I32), 0)
         nc.vector.memset(x_plane[:].bitcast(I32), 0)
-        nc.vector.memset(w3_plane[:].bitcast(I32), 0)
+        pass_plane = [tile("pass_plane%d" % o, [P, 2 * S], U8) for o in range(2)]
+        for plane in pass_plane + [w3_plane]:
+            nc.vector.memset(plane[:].bitcast(I32), 0)
 
-        passes = [(w2, e_words, 0, W, tok_sb, 8, 2), (w2, e_words, 1, W, tok_sb, 12, 2),
+        passes = [(w2, e_words, 0, W, tok_sb, 8, 4), (w2, e_words, 1, W, tok_sb, 12, 2),
                   (w1, x_words, 0, T, offs_sb, 0, 2), (w1, x_words, 1, T, offs_sb, 4, 4)]
 
         w_raw = [tile("w_raw%d" % g, [P, PACK, H], F32) for g in range(4)]
@@ -60,32 +62,15 @@ def tile_picked_zeagle_gelu_p_kernel(
             words, o = passes[g][1], passes[g][2]
             nc.sync.dma_start(out=table[g][:], in_=words[o].rearrange("p n t -> p (n t)").bitcast(I32))
 
-        def load_scale_rows(plane, first, scales, r):
-            nc.sync.dma_start(
-                out=plane[first + r : P : 32, :].bitcast(I32), in_=scales[r : 16 : QUADS, :].bitcast(I32)
-            )
-
-        rows = [(e_plane, 8 + 4 * o, e_scales[o], r) for r in range(4) for o in range(2)]
-        rows = rows + [(x_plane, 4 * o, x_scales[o], r) for r in range(4) for o in range(2)]
         load_w(0)
-        nc.sync.dma_start(offs_sb[:], offs)
         nc.sync.dma_start(tok_sb[:], tok)
-        for g, (first, last) in enumerate(((0, 4), (4, 10), (10, 16))):
-            for row in rows[first:last]:
-                load_scale_rows(*row)
-            load_w(g + 1)
-        for g in range(2):
-            load_table(g)
-            for r in range(2 * g, 2 * g + 2):
-                load_scale_rows(w3_plane, 0, w3_scales[0], r)
-        load_table(2)
-        load_table(3)
-        w3_sb = tile("w3_sb", [P, 2 * N], U8)
-        nc.sync.dma_start(out=w3_sb[:].bitcast(I32), in_=w3_words[0].bitcast(I32))
-        skip_view = skip.rearrange("(m p) j -> p m j", p=P)
-        skip_sb = [tile("skip_sb%d" % half, [P, N // P, S // 2], F32) for half in range(2)]
-        for half in range(2):
-            nc.sync.dma_start(out=skip_sb[half][:], in_=skip_view[:, :, half * S // 2 : (half + 1) * S // 2])
+        nc.sync.dma_start(offs_sb[:], offs)
+        for plane, scales in ((e_plane, e_scales), (x_plane, x_scales)):
+            nc.sync.dma_start(
+                out=plane[0:P:4, :].bitcast(I32), in_=scales.rearrange("o q c -> (o q) c").bitcast(I32)
+            )
+        for g in range(1, 4):
+            load_w(g)
 
         w_codes, w_plane = [], []
 
@@ -104,9 +89,6 @@ def tile_picked_zeagle_gelu_p_kernel(
                 in_=grouped[:].rearrange("p t m j -> p (t m j)"),
             )
 
-        x_picked_plane = tile("x_picked_plane", [P, S], U8)
-        e_picked_plane = tile("e_picked_plane", [P, S], U8)
-        picked_plane = [e_picked_plane, e_picked_plane, x_picked_plane, x_picked_plane]
         acc = [psum.tile([P, PACK, P], F32, name="acc%d" % c, tag="bank%d" % c) for c in range(CHUNKS)]
         picked = [tile("picked%d" % g, [P, S], U32) for g in range(4)]
 
@@ -129,16 +111,48 @@ def tile_picked_zeagle_gelu_p_kernel(
                         lhsT=w_codes[g][:, cols].bitcast(FP8X4),
                         lhsT_scale=w_plane[g][:, cols],
                         rhs=picked[g][:, nodes].bitcast(FP8X4),
-                        rhs_scale=picked_plane[g][passes[g][5] : P, nodes],
+                        rhs_scale=pass_plane[g % 2][4 * (g % 2) : P, g // 2 * S + c * P : g // 2 * S + (c + 1) * P],
                         start=(g == 0 and t == 0),
                         stop=(g == 3 and t == PACK - 1),
                     )
 
-        quantize_w(0, None)
-        nc.vector.tensor_copy(e_picked_plane[:], e_plane[:].indirect(tok_sb[:]))
-        quantize_w(1, "e_plane")
-        nc.vector.tensor_copy(x_picked_plane[:], x_plane[:].indirect(offs_sb[:]))
-        quantize_w(2, "x_plane")
+        picked_rows = tile("picked_rows", [P, 2 * S], U8)
+
+        def move_row(o, r):
+            nc.sync.dma_start(
+                out=pass_plane[o][4 * o + r : P : 32, :].bitcast(I32),
+                in_=picked_rows[64 * o + 4 * r : 64 * o + 64 : 16, :].bitcast(I32),
+            )
+
+        def load_w3_row(r):
+            nc.sync.dma_start(
+                out=w3_plane[r:P:32, :].bitcast(I32), in_=w3_scales[0][r : 16 : QUADS, :].bitcast(I32)
+            )
+
+        nc.vector.tensor_copy(picked_rows[:, :S], e_plane[:].indirect(tok_sb[:]))
+        quantize_w(0, "e_plane")
+        nc.vector.tensor_copy(picked_rows[:, S:], x_plane[:].indirect(offs_sb[:]))
+        quantize_w(1, "x_plane")
+        moves = [(o, r) for o in range(2) for r in range(4)]
+        for move in moves[:5]:
+            move_row(*move)
+        load_table(0)
+        load_table(1)
+        for move in moves[5:]:
+            move_row(*move)
+        load_table(2)
+        for r in range(4):
+            load_w3_row(r)
+        load_table(3)
+        w3_sb = tile("w3_sb", [P, 2 * N], U8)
+        nc.sync.dma_start(out=w3_sb[:].bitcast(I32), in_=w3_words[0].bitcast(I32))
+        skip_view = skip.rearrange("(m p) j -> p m j", p=P)
+        skip_sb = [tile("skip_sb%d" % half, [P, N // P, S // 2], F32) for half in range(2)]
+        for half in range(2):
+            nc.sync.dma_start(out=skip_sb[half][:], in_=skip_view[:, :, half * S // 2 : (half + 1) * S // 2])
+
+
+        quantize_w(2, None)
         gather(0)
         multiply(0)
         gather(1)

@@ -130,9 +130,9 @@ def tile_picked_zeagle_gelu_p_kernel(
             )
 
         nc.vector.tensor_copy(picked_rows[:, :S], e_plane[:].indirect(tok_sb[:]))
-        quantize_w(0, "e_plane")
         nc.vector.tensor_copy(picked_rows[:, S:], x_plane[:].indirect(offs_sb[:]))
-        quantize_w(1, "x_plane")
+        quantize_w(0, "x_plane")
+        quantize_w(1, None)
         moves = [(o, r) for o in range(2) for r in range(4)]
         for move in moves[:5]:
             move_row(*move)
@@ -225,5 +225,9 @@ def tile_picked_zeagle_gelu_p_kernel(
         finish(1, 1)
         quantize(3)
         second(3, 2)
-        finish(2, 1)
-        finish(3, 2)
+        pair = tile("result_pair", [P, N // P, 2 * P], F32)
+        nc.vector.tensor_tensor(pair[:, :, :P], y[(2, 0)][:], skip_sb[1][:, :, :P], ADD)
+        for part in range(2):
+            ms = slice(2 * part, 2 * part + 2)
+            nc.vector.tensor_tensor(pair[:, ms, P:], y[(3, part)][:], skip_sb[1][:, ms, P:], ADD)
+            nc.sync.dma_start(out=out_view[:, ms, 2 * P :], in_=pair[:, ms, :])

@@ -219,15 +219,15 @@ def tile_picked_zeagle_gelu_p_kernel(
         second(0, 2)
         quantize(1)
         second(1, 1)
-        finish(0, 2)
+        first = tile("result_first", [P, N // P, P], F32)
+        for part in range(2):
+            ms = slice(2 * part, 2 * part + 2)
+            nc.vector.tensor_tensor(first[:, ms, :], y[(0, part)][:], skip_sb[0][:, ms, :P], ADD)
+        nc.sync.dma_start(out=out_view[:, :, :P], in_=first[:])
         quantize(2)
         second(2, 1)
         finish(1, 1)
         quantize(3)
         second(3, 2)
-        pair = tile("result_pair", [P, N // P, 2 * P], F32)
-        nc.vector.tensor_tensor(pair[:, :, :P], y[(2, 0)][:], skip_sb[1][:, :, :P], ADD)
-        for part in range(2):
-            ms = slice(2 * part, 2 * part + 2)
-            nc.vector.tensor_tensor(pair[:, ms, P:], y[(3, part)][:], skip_sb[1][:, ms, P:], ADD)
-            nc.sync.dma_start(out=out_view[:, ms, 2 * P :], in_=pair[:, ms, :])
+        finish(2, 1)
+        finish(3, 2)

@@ -141,15 +141,16 @@ def tile_picked_zeagle_gelu_p_kernel(
         for move in moves[5:]:
             move_row(*move)
         load_table(2)
-        for r in range(4):
-            load_w3_row(r)
         load_table(3)
         w3_sb = tile("w3_sb", [P, 2 * N], U8)
-        nc.sync.dma_start(out=w3_sb[:].bitcast(I32), in_=w3_words[0].bitcast(I32))
         skip_view = skip.rearrange("(m p) j -> p m j", p=P)
         skip_sb = [tile("skip_sb%d" % half, [P, N // P, S // 2], F32) for half in range(2)]
         for half in range(2):
             nc.sync.dma_start(out=skip_sb[half][:], in_=skip_view[:, :, half * S // 2 : (half + 1) * S // 2])
+            if half == 0:
+                for r in range(4):
+                    load_w3_row(r)
+                nc.sync.dma_start(out=w3_sb[:].bitcast(I32), in_=w3_words[0].bitcast(I32))
 
 
         quantize_w(2, None)
@@ -165,7 +166,7 @@ def tile_picked_zeagle_gelu_p_kernel(
 
         out_view = out.rearrange("(m p) j -> p m j", p=P)
         h_grouped = [tile("h_grouped%d" % c, [P, P, PACK], BF16) for c in range(CHUNKS)]
-        h_codes = [tile("h_codes%d" % c, [P, P], U32) for c in range(CHUNKS)]
+        h_codes = []
         h_plane = [tile("h_plane%d" % c, [P, P], U8) for c in range(CHUNKS)]
         y = {}
         results = {}
@@ -178,6 +179,7 @@ def tile_picked_zeagle_gelu_p_kernel(
             )
 
         def quantize(c):
+            h_codes.append(tile("h_codes%d" % c, [P, P], U32, "h_codes%d" % (c % 2)))
             nc.vector.quantize_mx(
                 out=h_codes[c][:].bitcast(FP8X4),
                 scales=h_plane[c][:],

@@ -37,20 +37,19 @@ def tile_picked_zeagle_gelu_p_kernel(
 
         offs_sb = keep.tile([P, S // 16], U16, name="offs_sb")
         tok_sb = keep.tile([P, S // 16], U16, name="tok_sb")
-        x_plane = tile("x_plane", [P, T], U8)
-        e_plane = tile("e_plane", [P, W], U8)
+        e_rows = tile("e_rows", [P, W], U8)
+        x_rows = tile("x_rows", [P, T], U8)
         w3_plane = tile("w3_plane", [P, N], U8)
-        nc.vector.memset(e_plane[:].bitcast(I32), 0)
-        nc.vector.memset(x_plane[:].bitcast(I32), 0)
-        pass_plane = [tile("pass_plane%d" % o, [P, 2 * S], U8) for o in range(2)]
-        for plane in pass_plane + [w3_plane]:
-            nc.vector.memset(plane[:].bitcast(I32), 0)
+        for cleared in (e_rows, w3_plane, x_rows):
+            nc.gpsimd.memset(cleared[:].bitcast(I32), 0)
 
-        passes = [(w2, e_words, 0, W, tok_sb, 8, 4), (w2, e_words, 1, W, tok_sb, 12, 2),
-                  (w1, x_words, 0, T, offs_sb, 0, 2), (w1, x_words, 1, T, offs_sb, 4, 4)]
-
+        passes = [(w2, e_words, 0, tok_sb, 1), (w2, e_words, 1, tok_sb, 2),
+                  (w1, x_words, 0, offs_sb, 2), (w1, x_words, 1, offs_sb, 4)]
         w_raw = [tile("w_raw%d" % g, [P, PACK, H], F32) for g in range(4)]
-        table = [tile("table%d" % g, [P, passes[g][3]], I32) for g in range(4)]
+        table = [tile("table%d" % g, [P, passes[g][1].shape[2]], I32) for g in range(4)]
+        picked = [tile("picked%d" % g, [P, S], U32) for g in range(4)]
+        picked_rows = tile("picked_rows", [P, 2, S], U8)
+        plane = tile("plane", [P, 2, S], U8)
 
         def load_w(g):
             w, o = passes[g][0], passes[g][2]
@@ -62,15 +61,14 @@ def tile_picked_zeagle_gelu_p_kernel(
             words, o = passes[g][1], passes[g][2]
             nc.sync.dma_start(out=table[g][:], in_=words[o].rearrange("p n t -> p (n t)").bitcast(I32))
 
-        load_w(0)
-        nc.sync.dma_start(tok_sb[:], tok)
-        nc.sync.dma_start(offs_sb[:], offs)
-        for plane, scales in ((e_plane, e_scales), (x_plane, x_scales)):
-            nc.sync.dma_start(
-                out=plane[0:P:4, :].bitcast(I32), in_=scales.rearrange("o q c -> (o q) c").bitcast(I32)
-            )
-        for g in range(1, 4):
-            load_w(g)
+        def gather(g):
+            lst, pieces = passes[g][3], passes[g][4]
+            width = S // pieces
+            for piece in range(pieces):
+                nc.vector.tensor_copy(
+                    picked[g][:, piece * width : (piece + 1) * width],
+                    table[g][:].bitcast(U32).indirect(lst[:, piece * width // 16 : (piece + 1) * width // 16]),
+                )
 
         w_codes, w_plane = [], []
 
@@ -90,18 +88,9 @@ def tile_picked_zeagle_gelu_p_kernel(
             )
 
         acc = [psum.tile([P, PACK, P], F32, name="acc%d" % c, tag="bank%d" % c) for c in range(CHUNKS)]
-        picked = [tile("picked%d" % g, [P, S], U32) for g in range(4)]
-
-        def gather(g):
-            lst, pieces = passes[g][4], passes[g][6]
-            width = S // pieces
-            for piece in range(pieces):
-                nc.vector.tensor_copy(
-                    picked[g][:, piece * width : (piece + 1) * width],
-                    table[g][:].bitcast(U32).indirect(lst[:, piece * width // 16 : (piece + 1) * width // 16]),
-                )
 
         def multiply(g):
+            o = passes[g][2]
             for c in range(CHUNKS):
                 nodes = slice(c * P, (c + 1) * P)
                 for t in range(PACK):
@@ -111,37 +100,31 @@ def tile_picked_zeagle_gelu_p_kernel(
                         lhsT=w_codes[g][:, cols].bitcast(FP8X4),
                         lhsT_scale=w_plane[g][:, cols],
                         rhs=picked[g][:, nodes].bitcast(FP8X4),
-                        rhs_scale=pass_plane[g % 2][4 * (g % 2) : P, g // 2 * S + c * P : g // 2 * S + (c + 1) * P],
+                        rhs_scale=plane[4 * o : P, g // 2, nodes],
                         start=(g == 0 and t == 0),
                         stop=(g == 3 and t == PACK - 1),
                     )
 
-        picked_rows = tile("picked_rows", [P, 2 * S], U8)
-
-        def move_row(o, r):
-            nc.sync.dma_start(
-                out=pass_plane[o][4 * o + r : P : 32, :].bitcast(I32),
-                in_=picked_rows[64 * o + 4 * r : 64 * o + 64 : 16, :].bitcast(I32),
-            )
-
-        def load_w3_row(r):
-            nc.sync.dma_start(
-                out=w3_plane[r:P:32, :].bitcast(I32), in_=w3_scales[0][r : 16 : QUADS, :].bitcast(I32)
-            )
-
-        nc.vector.tensor_copy(picked_rows[:, :S], e_plane[:].indirect(tok_sb[:]))
-        nc.vector.tensor_copy(picked_rows[:, S:], x_plane[:].indirect(offs_sb[:]))
-        quantize_w(0, "x_plane")
-        quantize_w(1, None)
-        moves = [(o, r) for o in range(2) for r in range(4)]
-        for move in moves[:5]:
-            move_row(*move)
         load_table(0)
-        load_table(1)
-        for move in moves[5:]:
-            move_row(*move)
-        load_table(2)
-        load_table(3)
+        nc.sync.dma_start(tok_sb[:], tok)
+        nc.sync.dma_start(offs_sb[:], offs)
+        for rows, scales in ((e_rows, e_scales), (x_rows, x_scales)):
+            nc.sync.dma_start(out=rows[0:P:4, :].bitcast(I32), in_=scales.rearrange("o q c -> q o c").bitcast(I32))
+        for g in range(3):
+            load_w(g)
+
+        nc.vector.tensor_copy(picked_rows[:, 0, :], e_rows[:].indirect(tok_sb[:]))
+        nc.vector.tensor_copy(picked_rows[:, 1, :], x_rows[:].indirect(offs_sb[:]))
+        nc.vector.tensor_copy(plane[:].bitcast(I32), picked_rows[:].bitcast(I32))
+        moves = [(o, r) for r in range(1, 4) for o in range(2)]
+        for i, (o, r) in enumerate(moves):
+            if i == len(moves) - 1:
+                load_w(3)
+            nc.sync.dma_start(
+                out=plane[4 * o + r : P : 32].bitcast(I32), in_=picked_rows[4 * o + 8 * r : P : 32].bitcast(I32)
+            )
+        for g in range(1, 4):
+            load_table(g)
         w3_sb = tile("w3_sb", [P, 2 * N], U8)
         skip_view = skip.rearrange("(m p) j -> p m j", p=P)
         skip_sb = [tile("skip_sb%d" % half, [P, N // P, S // 2], F32) for half in range(2)]
@@ -149,13 +132,16 @@ def tile_picked_zeagle_gelu_p_kernel(
             nc.sync.dma_start(out=skip_sb[half][:], in_=skip_view[:, :, half * S // 2 : (half + 1) * S // 2])
             if half == 0:
                 for r in range(4):
-                    load_w3_row(r)
+                    nc.sync.dma_start(
+                        out=w3_plane[r:P:32, :].bitcast(I32), in_=w3_scales[0][r : 16 : QUADS, :].bitcast(I32)
+                    )
                 nc.sync.dma_start(out=w3_sb[:].bitcast(I32), in_=w3_words[0].bitcast(I32))
 
-
-        quantize_w(2, None)
         gather(0)
+        quantize_w(0, None)
         multiply(0)
+        quantize_w(1, None)
+        quantize_w(2, None)
         gather(1)
         multiply(1)
         quantize_w(3, "table1")

@@ -127,9 +127,10 @@ def tile_picked_zeagle_gelu_p_kernel(
             load_table(g)
         w3_sb = tile("w3_sb", [P, 2 * N], U8)
         skip_view = skip.rearrange("(m p) j -> p m j", p=P)
-        skip_sb = [tile("skip_sb%d" % half, [P, N // P, S // 2], F32) for half in range(2)]
+        skip_sb = tile("skip_sb", [P, N // P, S], F32)
         for half in range(2):
-            nc.sync.dma_start(out=skip_sb[half][:], in_=skip_view[:, :, half * S // 2 : (half + 1) * S // 2])
+            nodes = slice(half * S // 2, (half + 1) * S // 2)
+            nc.sync.dma_start(out=skip_sb[:, :, nodes], in_=skip_view[:, :, nodes])
             if half == 0:
                 for r in range(4):
                     nc.sync.dma_start(
@@ -152,10 +153,13 @@ def tile_picked_zeagle_gelu_p_kernel(
 
         out_view = out.rearrange("(m p) j -> p m j", p=P)
         h_grouped = [tile("h_grouped%d" % c, [P, P, PACK], BF16) for c in range(CHUNKS)]
-        h_codes = []
+        h_codes = [None] * CHUNKS
         h_plane = [tile("h_plane%d" % c, [P, P], U8) for c in range(CHUNKS)]
+
+        windows = [(0, 2, 0, 1), (2, 1, 0, 2), (3, 1, 0, 2), (0, 1, 1, 2), (1, 1, 1, 2),
+                   (2, 1, 2, 2), (3, 1, 2, 2), (0, 2, 3, 1)]
+        banks = ["out0", "out1", "out2", "out3", "bank0", "bank1", "bank2", "bank3"]
         y = {}
-        results = {}
 
         def gelu(c):
             nc.scalar.activation(
@@ -165,57 +169,55 @@ def tile_picked_zeagle_gelu_p_kernel(
             )
 
         def quantize(c):
-            h_codes.append(tile("h_codes%d" % c, [P, P], U32, "h_codes%d" % (c % 2)))
+            h_codes[c] = tile("h_codes%d" % c, [P, P], U32, "h_codes%d" % (c % 2))
             nc.vector.quantize_mx(
                 out=h_codes[c][:].bitcast(FP8X4),
                 scales=h_plane[c][:],
                 in_=h_grouped[c][:].rearrange("p j t -> p (j t)"),
             )
 
-        def second(c, parts):
-            rows = N // P // parts
-            for part in range(parts):
-                bank = psum.tile([P, rows, P], F32, name="y%d_%d" % (c, part), tag=("out%d", "bank%d")[part] % c)
-                y.setdefault((c, part), bank)
-                for i in range(rows):
-                    m = part * rows + i
-                    nc.tensor.matmul_mx(
-                        out=bank[:, i, :],
-                        lhsT=w3_sb[:, 2 * P * m : 2 * P * (m + 1)].bitcast(FP4X4),
-                        lhsT_scale=w3_plane[:, m * P : (m + 1) * P],
-                        rhs=h_codes[c][:].bitcast(FP8X4),
-                        rhs_scale=h_plane[c][:],
-                        start=True,
-                        stop=True,
-                    )
+        def second(c):
+            for i, (m0, rows, c0, chunks) in enumerate(windows):
+                if c0 <= c < c0 + chunks:
+                    if c == c0:
+                        y[i] = psum.tile([P, rows, chunks * P], F32, name="y%d" % i, tag=banks[i])
+                    for m in range(m0, m0 + rows):
+                        nc.tensor.matmul_mx(
+                            out=y[i][:, m - m0, (c - c0) * P : (c - c0 + 1) * P],
+                            lhsT=w3_sb[:, 2 * P * m : 2 * P * (m + 1)].bitcast(FP4X4),
+                            lhsT_scale=w3_plane[:, m * P : (m + 1) * P],
+                            rhs=h_codes[c][:].bitcast(FP8X4),
+                            rhs_scale=h_plane[c][:],
+                            start=True,
+                            stop=True,
+                        )
 
-        def finish(c, parts):
-            nodes = slice(c * P, (c + 1) * P)
-            rows = N // P // parts
-            for part in range(parts):
-                ms = slice(part * rows, (part + 1) * rows)
-                result = tile("result%d_%d" % (c, part), [P, rows, P], F32)
-                results.setdefault(c, result)
+        def finish(group):
+            m0, c0, chunks = windows[group[0]][0], windows[group[0]][2], windows[group[0]][3]
+            nodes = slice(c0 * P, (c0 + chunks) * P)
+            total = sum(windows[i][1] for i in group)
+            result = tile("result%d" % group[0], [P, total, chunks * P], F32)
+            for i in group:
+                m, rows = windows[i][0], windows[i][1]
                 nc.vector.tensor_tensor(
-                    result[:], y[(c, part)][:], skip_sb[c // 2][:, ms, c % 2 * P : (c % 2 + 1) * P], ADD
+                    result[:, m - m0 : m - m0 + rows, :], y[i][:], skip_sb[:, m : m + rows, nodes], ADD
                 )
-                nc.sync.dma_start(out=out_view[:, ms, nodes], in_=result[:])
+            nc.sync.dma_start(out=out_view[:, m0 : m0 + total, nodes], in_=result[:])
 
         for c in range(CHUNKS):
             gelu(c)
         quantize(0)
-        second(0, 2)
+        second(0)
         quantize(1)
-        second(1, 1)
-        first = tile("result_first", [P, N // P, P], F32)
-        for part in range(2):
-            ms = slice(2 * part, 2 * part + 2)
-            nc.vector.tensor_tensor(first[:, ms, :], y[(0, part)][:], skip_sb[0][:, ms, :P], ADD)
-        nc.sync.dma_start(out=out_view[:, :, :P], in_=first[:])
+        second(1)
+        finish([0])
         quantize(2)
-        second(2, 1)
-        finish(1, 1)
+        second(2)
+        finish([1])
+        finish([2])
         quantize(3)
-        second(3, 2)
-        finish(2, 1)
-        finish(3, 2)
+        second(3)
+        finish([3])
+        finish([4])
+        finish([5, 6])
+        finish([7])

@@ -21,7 +21,7 @@ PACK = 4
 K_PASS = P * PACK
 QUADS = 4
 CHUNKS = S // P
-SCALAR_SHARE = 80
+SCALAR_SHARE = 64
 
 
 def tile_picked_zeagle_gelu_p_kernel(
@@ -43,23 +43,24 @@ def tile_picked_zeagle_gelu_p_kernel(
         for cleared in (e_rows, w3_plane, x_rows):
             nc.gpsimd.memset(cleared[:].bitcast(I32), 0)
 
-        passes = [(w2, e_words, 0, tok_sb, 1), (w2, e_words, 1, tok_sb, 2),
+        passes = [(w2, e_words, 0, tok_sb, 1), (w2, e_words, 1, tok_sb, 1),
                   (w1, x_words, 0, offs_sb, 2), (w1, x_words, 1, offs_sb, 4)]
-        w_raw = [tile("w_raw%d" % g, [P, PACK, H], F32) for g in range(4)]
-        table = [tile("table%d" % g, [P, passes[g][1].shape[2]], I32) for g in range(4)]
-        picked = [tile("picked%d" % g, [P, S], U32) for g in range(4)]
+        w2_raw = tile("w2_raw", [P, 2, PACK, H], F32)
+        w_raw = [w2_raw[:, 0], w2_raw[:, 1]] + [tile("w_raw%d" % g, [P, PACK, H], F32)[:] for g in (2, 3)]
+        e_table = tile("e_table", [P, 2, W], I32)
+        table = [e_table[:, 0], e_table[:, 1]] + [tile("table%d" % g, [P, T], I32)[:] for g in (2, 3)]
         picked_rows = tile("picked_rows", [P, 2, S], U8)
-        plane = tile("plane", [P, 2, S], U8)
+        plane = tile("plane", [P, 3, S], U8)
 
         def load_w(g):
             w, o = passes[g][0], passes[g][2]
             nc.sync.dma_start(
-                out=w_raw[g][:], in_=w[o * K_PASS : (o + 1) * K_PASS, :].rearrange("(p t) c -> p t c", t=PACK)
+                out=w_raw[g], in_=w[o * K_PASS : (o + 1) * K_PASS, :].rearrange("(p t) c -> p t c", t=PACK)
             )
 
         def load_table(g):
             words, o = passes[g][1], passes[g][2]
-            nc.sync.dma_start(out=table[g][:], in_=words[o].rearrange("p n t -> p (n t)").bitcast(I32))
+            nc.sync.dma_start(out=table[g], in_=words[o].rearrange("p n t -> p (n t)").bitcast(I32))
 
         def gather(g):
             lst, pieces = passes[g][3], passes[g][4]
@@ -67,17 +68,17 @@ def tile_picked_zeagle_gelu_p_kernel(
             for piece in range(pieces):
                 nc.vector.tensor_copy(
                     picked[g][:, piece * width : (piece + 1) * width],
-                    table[g][:].bitcast(U32).indirect(lst[:, piece * width // 16 : (piece + 1) * width // 16]),
+                    table[g].bitcast(U32).indirect(lst[:, piece * width // 16 : (piece + 1) * width // 16]),
                 )
 
         w_codes, w_plane = [], []
 
         def quantize_w(g, after):
-            grouped = tile("w_grouped%d" % g, [P, PACK, P, PACK], BF16)
+            grouped = tile("w_grouped%d" % g, [P, PACK, P, PACK], BF16, "w_grouped%d" % (g % 2))
             for ms, copy in ((slice(0, SCALAR_SHARE), nc.scalar.copy), (slice(SCALAR_SHARE, P), nc.vector.tensor_copy)):
                 copy(
                     out=grouped[:, :, ms, :].rearrange("p t m j -> p m j t"),
-                    in_=w_raw[g][:].rearrange("p j (m t) -> p m j t", t=PACK)[:, ms],
+                    in_=w_raw[g].rearrange("p j (m t) -> p m j t", t=PACK)[:, ms],
                 )
             w_codes.append(tile("w_codes%d" % g, [P, H], U32, after))
             w_plane.append(tile("w_plane%d" % g, [P, H], U8))
@@ -100,52 +101,62 @@ def tile_picked_zeagle_gelu_p_kernel(
                         lhsT=w_codes[g][:, cols].bitcast(FP8X4),
                         lhsT_scale=w_plane[g][:, cols],
                         rhs=picked[g][:, nodes].bitcast(FP8X4),
-                        rhs_scale=plane[4 * o : P, g // 2, nodes],
+                        rhs_scale=plane[4 * o : P, max(g - 1, 0), nodes],
                         start=(g == 0 and t == 0),
                         stop=(g == 3 and t == PACK - 1),
                     )
 
-        load_table(0)
+        nc.sync.dma_start(out=e_table[:], in_=e_words.rearrange("o p n t -> p o (n t)").bitcast(I32))
         nc.sync.dma_start(tok_sb[:], tok)
         nc.sync.dma_start(offs_sb[:], offs)
         for rows, scales in ((e_rows, e_scales), (x_rows, x_scales)):
             nc.sync.dma_start(out=rows[0:P:4, :].bitcast(I32), in_=scales.rearrange("o q c -> q o c").bitcast(I32))
-        for g in range(3):
-            load_w(g)
+        nc.sync.dma_start(
+            out=w2_raw[:].rearrange("p o t c -> p o (t c)"), in_=w2.rearrange("(o p t) c -> p o (t c)", o=2, t=PACK)
+        )
+        load_w(2)
 
         nc.vector.tensor_copy(picked_rows[:, 0, :], e_rows[:].indirect(tok_sb[:]))
         nc.vector.tensor_copy(picked_rows[:, 1, :], x_rows[:].indirect(offs_sb[:]))
-        nc.vector.tensor_copy(plane[:].bitcast(I32), picked_rows[:].bitcast(I32))
+        nc.vector.tensor_copy(plane[:, 0:2].bitcast(I32), picked_rows[:].bitcast(I32))
+        nc.vector.tensor_copy(plane[:, 2].bitcast(I32), picked_rows[:, 1].bitcast(I32))
         moves = [(o, r) for r in range(1, 4) for o in range(2)]
-        for i, (o, r) in enumerate(moves):
-            if i == len(moves) - 1:
-                load_w(3)
+
+        def move(o, r, tables, slots=None):
             nc.sync.dma_start(
-                out=plane[4 * o + r : P : 32].bitcast(I32), in_=picked_rows[4 * o + 8 * r : P : 32].bitcast(I32)
+                out=plane[4 * o + r : P : 32, slots or tables].bitcast(I32),
+                in_=picked_rows[4 * o + 8 * r : P : 32, tables].bitcast(I32),
             )
-        for g in range(1, 4):
-            load_table(g)
+
+        for o, r in moves:
+            move(o, r, slice(0, 2) if o == 0 and r > 1 else slice(0, 1))
+        load_w(3)
+        load_table(2)
+        move(0, 1, slice(1, 2))
+        load_table(3)
+        for r in range(1, 4):
+            move(1, r, slice(1, 2), slice(2, 3))
         w3_sb = tile("w3_sb", [P, 2 * N], U8)
         skip_view = skip.rearrange("(m p) j -> p m j", p=P)
-        skip_sb = tile("skip_sb", [P, N // P, S], F32)
+        skip_sb = [tile("skip_sb%d" % half, [P, N // P, S // 2], F32) for half in range(2)]
         for half in range(2):
-            nodes = slice(half * S // 2, (half + 1) * S // 2)
-            nc.sync.dma_start(out=skip_sb[:, :, nodes], in_=skip_view[:, :, nodes])
+            nc.sync.dma_start(out=skip_sb[half][:], in_=skip_view[:, :, half * S // 2 : (half + 1) * S // 2])
             if half == 0:
+                nc.sync.dma_start(out=w3_sb[:].bitcast(I32), in_=w3_words[0].bitcast(I32))
                 for r in range(4):
                     nc.sync.dma_start(
                         out=w3_plane[r:P:32, :].bitcast(I32), in_=w3_scales[0][r : 16 : QUADS, :].bitcast(I32)
                     )
-                nc.sync.dma_start(out=w3_sb[:].bitcast(I32), in_=w3_words[0].bitcast(I32))
 
+        picked_e = tile("picked_e", [P, 2, S], U32, "x_rows")
+        picked = [picked_e[:, 0], picked_e[:, 1]] + [tile("picked%d" % g, [P, S], U32)[:] for g in (2, 3)]
         gather(0)
-        quantize_w(0, None)
-        multiply(0)
-        quantize_w(1, None)
-        quantize_w(2, None)
         gather(1)
-        multiply(1)
-        quantize_w(3, "table1")
+        for g in range(2):
+            quantize_w(g, None)
+            multiply(g)
+        quantize_w(2, None)
+        quantize_w(3, None)
         gather(2)
         multiply(2)
         gather(3)
@@ -156,9 +167,8 @@ def tile_picked_zeagle_gelu_p_kernel(
         h_codes = [None] * CHUNKS
         h_plane = [tile("h_plane%d" % c, [P, P], U8) for c in range(CHUNKS)]
 
-        windows = [(0, 2, 0, 1), (2, 1, 0, 2), (3, 1, 0, 2), (0, 1, 1, 2), (1, 1, 1, 2),
-                   (2, 1, 2, 2), (3, 1, 2, 2), (0, 2, 3, 1)]
-        banks = ["out0", "out1", "out2", "out3", "bank0", "bank1", "bank2", "bank3"]
+        windows = [(0, 2, 0, 1), (2, 2, 0, 1), (0, 4, 1, 1), (0, 3, 2, 1), (3, 1, 2, 2), (0, 3, 3, 1)]
+        banks = ["out0", "bank0", "out1", "out2", "out3", "bank1"]
         y = {}
 
         def gelu(c):
@@ -200,7 +210,7 @@ def tile_picked_zeagle_gelu_p_kernel(
             for i in group:
                 m, rows = windows[i][0], windows[i][1]
                 nc.vector.tensor_tensor(
-                    result[:, m - m0 : m - m0 + rows, :], y[i][:], skip_sb[:, m : m + rows, nodes], ADD
+                    result[:, m - m0 : m - m0 + rows, :], y[i][:], skip_sb[c0 // 2][:, m : m + rows, c0 % 2 * P : (c0 % 2 + chunks) * P], ADD
                 )
             nc.sync.dma_start(out=out_view[:, m0 : m0 + total, nodes], in_=result[:])
 
@@ -210,14 +220,12 @@ def tile_picked_zeagle_gelu_p_kernel(
         second(0)
         quantize(1)
         second(1)
-        finish([0])
+        finish([0, 1])
         quantize(2)
         second(2)
-        finish([1])
         finish([2])
         quantize(3)
         second(3)
         finish([3])
         finish([4])
-        finish([5, 6])
-        finish([7])
+        finish([5])

from contextlib import ExitStack

import concourse.mybir as mybir

K, T, S, W, H, N = 1024, 2048, 512, 1024, 512, 512
FLOPS = 2 * (2 * K * H * S + H * N * S)

F32 = mybir.dt.float32
BF16 = mybir.dt.bfloat16
I32 = mybir.dt.int32
U32 = mybir.dt.uint32
U16 = mybir.dt.uint16
U8 = mybir.dt.uint8
FP8X4 = mybir.dt.float8_e4m3fn_x4
FP4X4 = mybir.dt.float4_e2m1fn_x4
GELU = mybir.ActivationFunctionType.Gelu_apprx_tanh
ADD = mybir.AluOpType.add

P = 128
PACK = 4
K_PASS = P * PACK
QUADS = 4
CHUNKS = S // P
SCALAR_SHARE = 64


def tile_picked_zeagle_gelu_p_kernel(
    tc, x_words, x_scales, e_words, e_scales, w1, w2, w3_words, w3_scales, skip, offs, tok, out
):
    nc = tc.nc
    with ExitStack() as ctx:
        keep = ctx.enter_context(tc.tile_pool(name="keep", bufs=1))
        psum = ctx.enter_context(tc.psum_pool(name="psum", bufs=1))

        def tile(name, shape, dtype, tag=None):
            return keep.tile(shape, dtype, name=name, tag=tag or name, align_bytes=1024)

        offs_sb = keep.tile([P, S // 16], U16, name="offs_sb")
        tok_sb = keep.tile([P, S // 16], U16, name="tok_sb")
        e_rows = tile("e_rows", [P, W], U8)
        x_rows = tile("x_rows", [P, T], U8)
        w3_plane = tile("w3_plane", [P, N], U8)
        for cleared in (e_rows, w3_plane, x_rows):
            nc.gpsimd.memset(cleared[:].bitcast(I32), 0)

        passes = [(w2, e_words, 0, tok_sb, 1), (w2, e_words, 1, tok_sb, 1),
                  (w1, x_words, 0, offs_sb, 2), (w1, x_words, 1, offs_sb, 4)]
        w2_raw = tile("w2_raw", [P, 2, PACK, H], F32)
        w_raw = [w2_raw[:, 0], w2_raw[:, 1]] + [tile("w_raw%d" % g, [P, PACK, H], F32)[:] for g in (2, 3)]
        e_table = tile("e_table", [P, 2, W], I32)
        table = [e_table[:, 0], e_table[:, 1]] + [tile("table%d" % g, [P, T], I32)[:] for g in (2, 3)]
        picked_rows = tile("picked_rows", [P, 2, S], U8)
        plane = tile("plane", [P, 3, S], U8)

        def load_w(g):
            w, o = passes[g][0], passes[g][2]
            nc.sync.dma_start(
                out=w_raw[g], in_=w[o * K_PASS : (o + 1) * K_PASS, :].rearrange("(p t) c -> p t c", t=PACK)
            )

        def load_table(g):
            words, o = passes[g][1], passes[g][2]
            nc.sync.dma_start(out=table[g], in_=words[o].rearrange("p n t -> p (n t)").bitcast(I32))

        def gather(g):
            lst, pieces = passes[g][3], passes[g][4]
            width = S // pieces
            for piece in range(pieces):
                nc.vector.tensor_copy(
                    picked[g][:, piece * width : (piece + 1) * width],
                    table[g].bitcast(U32).indirect(lst[:, piece * width // 16 : (piece + 1) * width // 16]),
                )

        w_codes, w_plane = [], []

        def quantize_w(g, after):
            grouped = tile("w_grouped%d" % g, [P, PACK, P, PACK], BF16, "w_grouped%d" % (g % 2))
            for ms, copy in ((slice(0, SCALAR_SHARE), nc.scalar.copy), (slice(SCALAR_SHARE, P), nc.vector.tensor_copy)):
                copy(
                    out=grouped[:, :, ms, :].rearrange("p t m j -> p m j t"),
                    in_=w_raw[g].rearrange("p j (m t) -> p m j t", t=PACK)[:, ms],
                )
            w_codes.append(tile("w_codes%d" % g, [P, H], U32, after))
            w_plane.append(tile("w_plane%d" % g, [P, H], U8))
            nc.vector.quantize_mx(
                out=w_codes[g][:].bitcast(FP8X4),
                scales=w_plane[g][:],
                in_=grouped[:].rearrange("p t m j -> p (t m j)"),
            )

        acc = [psum.tile([P, PACK, P], F32, name="acc%d" % c, tag="bank%d" % c) for c in range(CHUNKS)]

        def multiply(g):
            o = passes[g][2]
            for c in range(CHUNKS):
                nodes = slice(c * P, (c + 1) * P)
                for t in range(PACK):
                    cols = slice(t * P, (t + 1) * P)
                    nc.tensor.matmul_mx(
                        out=acc[c][:, t, :],
                        lhsT=w_codes[g][:, cols].bitcast(FP8X4),
                        lhsT_scale=w_plane[g][:, cols],
                        rhs=picked[g][:, nodes].bitcast(FP8X4),
                        rhs_scale=plane[4 * o : P, max(g - 1, 0), nodes],
                        start=(g == 0 and t == 0),
                        stop=(g == 3 and t == PACK - 1),
                    )

        nc.sync.dma_start(out=e_table[:], in_=e_words.rearrange("o p n t -> p o (n t)").bitcast(I32))
        nc.sync.dma_start(tok_sb[:], tok)
        nc.sync.dma_start(offs_sb[:], offs)
        for rows, scales in ((e_rows, e_scales), (x_rows, x_scales)):
            nc.sync.dma_start(out=rows[0:P:4, :].bitcast(I32), in_=scales.rearrange("o q c -> q o c").bitcast(I32))
        nc.sync.dma_start(
            out=w2_raw[:].rearrange("p o t c -> p o (t c)"), in_=w2.rearrange("(o p t) c -> p o (t c)", o=2, t=PACK)
        )
        load_w(2)

        nc.vector.tensor_copy(picked_rows[:, 0, :], e_rows[:].indirect(tok_sb[:]))
        nc.vector.tensor_copy(picked_rows[:, 1, :], x_rows[:].indirect(offs_sb[:]))
        nc.vector.tensor_copy(plane[:, 0:2].bitcast(I32), picked_rows[:].bitcast(I32))
        nc.vector.tensor_copy(plane[:, 2].bitcast(I32), picked_rows[:, 1].bitcast(I32))
        moves = [(o, r) for r in range(1, 4) for o in range(2)]

        def move(o, r, tables, slots=None):
            nc.sync.dma_start(
                out=plane[4 * o + r : P : 32, slots or tables].bitcast(I32),
                in_=picked_rows[4 * o + 8 * r : P : 32, tables].bitcast(I32),
            )

        for o, r in moves:
            move(o, r, slice(0, 2) if o == 0 and r > 1 else slice(0, 1))
        load_w(3)
        load_table(2)
        move(0, 1, slice(1, 2))
        load_table(3)
        for r in range(1, 4):
            move(1, r, slice(1, 2), slice(2, 3))
        w3_sb = tile("w3_sb", [P, 2 * N], U8)
        skip_view = skip.rearrange("(m p) j -> p m j", p=P)
        skip_sb = [tile("skip_sb%d" % half, [P, N // P, S // 2], F32) for half in range(2)]
        for half in range(2):
            nc.sync.dma_start(out=skip_sb[half][:], in_=skip_view[:, :, half * S // 2 : (half + 1) * S // 2])
            if half == 0:
                nc.sync.dma_start(out=w3_sb[:].bitcast(I32), in_=w3_words[0].bitcast(I32))
                for r in range(4):
                    nc.sync.dma_start(
                        out=w3_plane[r:P:32, :].bitcast(I32), in_=w3_scales[0][r : 16 : QUADS, :].bitcast(I32)
                    )

        picked_e = tile("picked_e", [P, 2, S], U32, "x_rows")
        picked = [picked_e[:, 0], picked_e[:, 1]] + [tile("picked%d" % g, [P, S], U32)[:] for g in (2, 3)]
        gather(0)
        gather(1)
        for g in range(2):
            quantize_w(g, None)
            multiply(g)
        quantize_w(2, None)
        quantize_w(3, None)
        gather(2)
        multiply(2)
        gather(3)
        multiply(3)

        out_view = out.rearrange("(m p) j -> p m j", p=P)
        h_grouped = [tile("h_grouped%d" % c, [P, P, PACK], BF16) for c in range(CHUNKS)]
        h_codes = [None] * CHUNKS
        h_plane = [tile("h_plane%d" % c, [P, P], U8) for c in range(CHUNKS)]

        windows = [(0, 2, 0, 1), (2, 2, 0, 1), (0, 4, 1, 1), (0, 3, 2, 1), (3, 1, 2, 2), (0, 3, 3, 1)]
        banks = ["out0", "bank0", "out1", "out2", "out3", "bank1"]
        y = {}

        def gelu(c):
            nc.scalar.activation(
                h_grouped[c][:].rearrange("p (j u) t -> p j t u", u=2),
                acc[c][:].rearrange("p t (j u) -> p j t u", u=2),
                GELU,
            )

        def quantize(c):
            h_codes[c] = tile("h_codes%d" % c, [P, P], U32, "h_codes%d" % (c % 2))
            nc.vector.quantize_mx(
                out=h_codes[c][:].bitcast(FP8X4),
                scales=h_plane[c][:],
                in_=h_grouped[c][:].rearrange("p j t -> p (j t)"),
            )

        def second(c):
            for i, (m0, rows, c0, chunks) in enumerate(windows):
                if c0 <= c < c0 + chunks:
                    if c == c0:
                        y[i] = psum.tile([P, rows, chunks * P], F32, name="y%d" % i, tag=banks[i])
                    for m in range(m0, m0 + rows):
                        nc.tensor.matmul_mx(
                            out=y[i][:, m - m0, (c - c0) * P : (c - c0 + 1) * P],
                            lhsT=w3_sb[:, 2 * P * m : 2 * P * (m + 1)].bitcast(FP4X4),
                            lhsT_scale=w3_plane[:, m * P : (m + 1) * P],
                            rhs=h_codes[c][:].bitcast(FP8X4),
                            rhs_scale=h_plane[c][:],
                            start=True,
                            stop=True,
                        )

        def finish(group):
            m0, c0, chunks = windows[group[0]][0], windows[group[0]][2], windows[group[0]][3]
            nodes = slice(c0 * P, (c0 + chunks) * P)
            total = sum(windows[i][1] for i in group)
            result = tile("result%d" % group[0], [P, total, chunks * P], F32)
            for i in group:
                m, rows = windows[i][0], windows[i][1]
                nc.vector.tensor_tensor(
                    result[:, m - m0 : m - m0 + rows, :], y[i][:], skip_sb[c0 // 2][:, m : m + rows, c0 % 2 * P : (c0 % 2 + chunks) * P], ADD
                )
            nc.sync.dma_start(out=out_view[:, m0 : m0 + total, nodes], in_=result[:])

        for c in range(CHUNKS):
            gelu(c)
        quantize(0)
        second(0)
        quantize(1)
        second(1)
        finish([0, 1])
        quantize(2)
        second(2)
        finish([2])
        quantize(3)
        second(3)
        finish([3])
        finish([4])
        finish([5])
